import numpy as np, ml_dtypes
CORES = [3,11,19,27,35,43,51,59,67,75,83,91]
N = 12
ROOT = 9
WIDTHS = [10,512,512,10,512,512,256,256,512,256,256,512]
XW = 512
def setup_inputs(rng):
    return {"x": rng.standard_normal((N, 128, XW), dtype=np.float32).astype(ml_dtypes.bfloat16)}
def reference(x):
    g = np.concatenate([x[r][:, :WIDTHS[r]] for r in range(N)], axis=1)
    y = np.full((N, 128, g.shape[1]), np.nan, x.dtype)
    y[ROOT] = g
    return {"y": y}

@@ -1,0 +1,104 @@
+ROOT_RANK = 9
+
+FLOWS = [
+    (0, 0, 10, []),
+    (1, 0, 256, []), (1, 256, 512, []),
+    (2, 256, 512, [70]), (2, 0, 256, [71]),
+    (3, 0, 10, []),
+    (4, 0, 256, [66]), (4, 256, 512, [66]),
+    (5, 256, 512, []), (5, 0, 256, []),
+    (6, 0, 256, [62]),
+    (7, 0, 256, [63]),
+    (8, 0, 512, []),
+    (10, 0, 256, []),
+    (11, 0, 512, [95]),
+]
+GROUPS = [
+    (2580, 3348, "g"),
+    (0, 266, "sync"),
+    (778, 1300, "scalar"),
+    (1812, 2580, "sync"),
+    (3348, 4116, "scalar"),
+    (266, 778, "sync"),
+    (1300, 1812, "scalar"),
+]
+
+SCRATCH = {
+    "land": ("sbuf", [128, 4116], "bfloat16"),
+}
+SEMAPHORES = (["f%d" % i for i in range(len(FLOWS))]
+              + ["grp%d" % j for j in range(len(GROUPS))]
+              + ["ld0", "ld1", "sent", "done_g", "done_h"])
+
+
+def rank_program(g, core, T, topo):
+    widths = T.tables["WIDTHS"]
+    cores = list(T.cores)
+    root = cores[ROOT_RANK]
+    off = [0]
+    for w in widths:
+        off.append(off[-1] + w)
+
+    def engines(src, dst):
+        m = topo.mask(src, dst)
+        return m, (16 if m == 0xFFFF else 8)
+
+    def group_of(a, b):
+        for j, (ga, gb, _q) in enumerate(GROUPS):
+            if ga <= a and b <= gb:
+                return j
+        raise ValueError("piece outside every store group")
+
+    sent = [0]
+
+    def send(i, a, b, dst):
+        m, n = engines(core, dst)
+        rid, pid, _se = topo.addr(dst)
+        rsem = T.sem["grp%d" % group_of(a, b)] if dst == root else T.sem["f%d" % i]
+        g.remote_dma(T.land[:, a:b], T.land[:, a:b], rsem, T.sem.sent, pid, rid, m)
+        sent[0] += n
+
+    if core == root:
+        a = off[ROOT_RANK]
+        b = a + widths[ROOT_RANK]
+        need = [0] * len(GROUPS)
+        need[group_of(a, b)] += 16
+        g.sync.dma_start(T.land[:, a:b], T.x[:, 0:widths[ROOT_RANK]]).then_inc(T.sem["grp%d" % group_of(a, b)], 16)
+        for (r, c0, c1, via) in FLOWS:
+            last = via[-1] if via else cores[r]
+            need[group_of(off[r] + c0, off[r] + c1)] += engines(last, root)[1]
+        n_g = 0
+        n_h = 0
+        for j, (ga, gb, qn) in enumerate(GROUPS):
+            q = g if qn == "g" else (g.sync if qn == "sync" else g.scalar)
+            q.wait_ge(T.sem["grp%d" % j], need[j])
+            if qn == "g":
+                q.dma_start(T.y[:, ga:gb], T.land[:, ga:gb]).then_inc(T.sem.done_g, 16)
+                n_g += 16
+            else:
+                q.dma_start(T.y[:, ga:gb], T.land[:, ga:gb]).then_inc(T.sem.done_h, 16)
+                n_h += 16
+        if n_g:
+            g.wait_ge(T.sem.done_g, n_g)
+        g.wait_ge(T.sem.done_h, n_h)
+        return
+
+    rank = T.rank_of(core)
+    if rank is not None:
+        mine = [(i, f) for i, f in enumerate(FLOWS) if f[0] == rank]
+        for k, (i, (r, c0, c1, via)) in enumerate(mine):
+            q = g.sync if k % 2 == 0 else g.scalar
+            q.dma_start(T.land[:, off[r] + c0:off[r] + c1], T.x[:, c0:c1]).then_inc(T.sem["ld%d" % k], 16)
+        for k, (i, (r, c0, c1, via)) in enumerate(mine):
+            g.wait_ge(T.sem["ld%d" % k], 16)
+            send(i, off[r] + c0, off[r] + c1, via[0] if via else root)
+    else:
+        for i, (r, c0, c1, via) in enumerate(FLOWS):
+            if core in via:
+                h = via.index(core)
+                prev = via[h - 1] if h else cores[r]
+                nxt = via[h + 1] if h + 1 < len(via) else root
+                g.wait_ge(T.sem["f%d" % i], engines(prev, core)[1])
+                send(i, off[r] + c0, off[r] + c1, nxt)
+    if sent[0]:
+        g.wait_ge(T.sem.sent, sent[0])

@@ -5,26 +5,31 @@ FLOWS = [
     (1, 0, 256, []), (1, 256, 512, []),
     (2, 256, 512, [70]), (2, 0, 256, [71]),
     (3, 0, 10, []),
-    (4, 0, 256, [66]), (4, 256, 512, [66]),
+    (4, 0, 256, [46]), (4, 256, 512, [47]),
     (5, 256, 512, []), (5, 0, 256, []),
-    (6, 0, 256, [62]),
-    (7, 0, 256, [63]),
+    (6, 0, 256, [66]),
+    (7, 0, 256, []),
     (8, 0, 512, []),
     (10, 0, 256, []),
     (11, 0, 512, [95]),
 ]
 GROUPS = [
-    (2580, 3348, "g"),
-    (0, 266, "sync"),
-    (778, 1300, "scalar"),
-    (1812, 2580, "sync"),
-    (3348, 4116, "scalar"),
-    (266, 778, "sync"),
-    (1300, 1812, "scalar"),
+    (2580, 3092, "sync"),
+    (0, 266, "scalar"),
+    (3348, 3604, "sync"),
+    (1812, 2068, "scalar"),
+    (778, 1300, "sync"),
+    (2068, 2580, "scalar"),
+    (3604, 4116, "sync"),
+    (266, 778, "scalar"),
+    (1300, 1812, "sync"),
 ]
 
 SCRATCH = {
     "land": ("sbuf", [128, 4116], "bfloat16"),
+    "d0": ("dram", [128, 256], "bfloat16"),
+    "d1": ("dram", [128, 256], "bfloat16"),
+    "dw": ("dram", [128, 512], "bfloat16"),
 }
 SEMAPHORES = (["f%d" % i for i in range(len(FLOWS))]
               + ["grp%d" % j for j in range(len(GROUPS))]
@@ -33,6 +38,7 @@ SEMAPHORES = (["f%d" % i for i in range(len(FLOWS))]
 
 def rank_program(g, core, T, topo):
     widths = T.tables["WIDTHS"]
+    xw = T.tables["XW"]
     cores = list(T.cores)
     root = cores[ROOT_RANK]
     off = [0]
@@ -49,49 +55,55 @@ def rank_program(g, core, T, topo):
                 return j
         raise ValueError("piece outside every store group")
 
+    def stage(i):
+        r, c0, c1, via = FLOWS[i]
+        k = [j for j, f in enumerate(FLOWS) if f[0] == r].index(i)
+        if c1 - c0 == xw:
+            return T.dw[:, :]
+        if via and c1 - c0 == 256:
+            return T.d0[:, :] if k == 0 else T.d1[:, :]
+        return T.land[:, off[r] + c0:off[r] + c1]
+
     sent = [0]
 
-    def send(i, a, b, dst):
+    def send(i, dst):
+        r, c0, c1, via = FLOWS[i]
+        a, b = off[r] + c0, off[r] + c1
         m, n = engines(core, dst)
         rid, pid, _se = topo.addr(dst)
-        rsem = T.sem["grp%d" % group_of(a, b)] if dst == root else T.sem["f%d" % i]
-        g.remote_dma(T.land[:, a:b], T.land[:, a:b], rsem, T.sem.sent, pid, rid, m)
+        if dst == root:
+            g.remote_dma(T.land[:, a:b], stage(i), T.sem["grp%d" % group_of(a, b)], T.sem.sent, pid, rid, m)
+        else:
+            g.remote_dma(stage(i), stage(i), T.sem["f%d" % i], T.sem.sent, pid, rid, m)
         sent[0] += n
 
     if core == root:
         a = off[ROOT_RANK]
-        b = a + widths[ROOT_RANK]
+        w = widths[ROOT_RANK]
+        g.dma_start(T.y[:, a:a + w], T.x[:, 0:w]).then_inc(T.sem.done_g, 16)
         need = [0] * len(GROUPS)
-        need[group_of(a, b)] += 16
-        g.sync.dma_start(T.land[:, a:b], T.x[:, 0:widths[ROOT_RANK]]).then_inc(T.sem["grp%d" % group_of(a, b)], 16)
         for (r, c0, c1, via) in FLOWS:
             last = via[-1] if via else cores[r]
             need[group_of(off[r] + c0, off[r] + c1)] += engines(last, root)[1]
-        n_g = 0
         n_h = 0
         for j, (ga, gb, qn) in enumerate(GROUPS):
-            q = g if qn == "g" else (g.sync if qn == "sync" else g.scalar)
+            q = g.sync if qn == "sync" else g.scalar
             q.wait_ge(T.sem["grp%d" % j], need[j])
-            if qn == "g":
-                q.dma_start(T.y[:, ga:gb], T.land[:, ga:gb]).then_inc(T.sem.done_g, 16)
-                n_g += 16
-            else:
-                q.dma_start(T.y[:, ga:gb], T.land[:, ga:gb]).then_inc(T.sem.done_h, 16)
-                n_h += 16
-        if n_g:
-            g.wait_ge(T.sem.done_g, n_g)
+            q.dma_start(T.y[:, ga:gb], T.land[:, ga:gb]).then_inc(T.sem.done_h, 16)
+            n_h += 16
+        g.wait_ge(T.sem.done_g, 16)
         g.wait_ge(T.sem.done_h, n_h)
         return
 
     rank = T.rank_of(core)
     if rank is not None:
-        mine = [(i, f) for i, f in enumerate(FLOWS) if f[0] == rank]
-        for k, (i, (r, c0, c1, via)) in enumerate(mine):
+        mine = [i for i, f in enumerate(FLOWS) if f[0] == rank]
+        for k, i in enumerate(mine):
             q = g.sync if k % 2 == 0 else g.scalar
-            q.dma_start(T.land[:, off[r] + c0:off[r] + c1], T.x[:, c0:c1]).then_inc(T.sem["ld%d" % k], 16)
-        for k, (i, (r, c0, c1, via)) in enumerate(mine):
+            q.dma_start(stage(i), T.x[:, FLOWS[i][1]:FLOWS[i][2]]).then_inc(T.sem["ld%d" % k], 16)
+        for k, i in enumerate(mine):
             g.wait_ge(T.sem["ld%d" % k], 16)
-            send(i, off[r] + c0, off[r] + c1, via[0] if via else root)
+            send(i, FLOWS[i][3][0] if FLOWS[i][3] else root)
     else:
         for i, (r, c0, c1, via) in enumerate(FLOWS):
             if core in via:
@@ -99,6 +111,6 @@ def rank_program(g, core, T, topo):
                 prev = via[h - 1] if h else cores[r]
                 nxt = via[h + 1] if h + 1 < len(via) else root
                 g.wait_ge(T.sem["f%d" % i], engines(prev, core)[1])
-                send(i, off[r] + c0, off[r] + c1, nxt)
+                send(i, nxt)
     if sent[0]:
         g.wait_ge(T.sem.sent, sent[0])

ROOT_RANK = 9

FLOWS = [
    (0, 0, 10, []),
    (1, 0, 256, []), (1, 256, 512, []),
    (2, 256, 512, [70]), (2, 0, 256, [71]),
    (3, 0, 10, []),
    (4, 0, 256, [46]), (4, 256, 512, [47]),
    (5, 256, 512, []), (5, 0, 256, []),
    (6, 0, 256, [66]),
    (7, 0, 256, []),
    (8, 0, 512, []),
    (10, 0, 256, []),
    (11, 0, 512, [95]),
]
GROUPS = [
    (2580, 3092, "sync"),
    (0, 266, "scalar"),
    (3348, 3604, "sync"),
    (1812, 2068, "scalar"),
    (778, 1300, "sync"),
    (2068, 2580, "scalar"),
    (3604, 4116, "sync"),
    (266, 778, "scalar"),
    (1300, 1812, "sync"),
]

SCRATCH = {
    "land": ("sbuf", [128, 4116], "bfloat16"),
    "d0": ("dram", [128, 256], "bfloat16"),
    "d1": ("dram", [128, 256], "bfloat16"),
    "dw": ("dram", [128, 512], "bfloat16"),
}
SEMAPHORES = (["f%d" % i for i in range(len(FLOWS))]
              + ["grp%d" % j for j in range(len(GROUPS))]
              + ["ld0", "ld1", "sent", "done_g", "done_h"])


def rank_program(g, core, T, topo):
    widths = T.tables["WIDTHS"]
    xw = T.tables["XW"]
    cores = list(T.cores)
    root = cores[ROOT_RANK]
    off = [0]
    for w in widths:
        off.append(off[-1] + w)

    def engines(src, dst):
        m = topo.mask(src, dst)
        return m, (16 if m == 0xFFFF else 8)

    def group_of(a, b):
        for j, (ga, gb, _q) in enumerate(GROUPS):
            if ga <= a and b <= gb:
                return j
        raise ValueError("piece outside every store group")

    def stage(i):
        r, c0, c1, via = FLOWS[i]
        k = [j for j, f in enumerate(FLOWS) if f[0] == r].index(i)
        if c1 - c0 == xw:
            return T.dw[:, :]
        if via and c1 - c0 == 256:
            return T.d0[:, :] if k == 0 else T.d1[:, :]
        return T.land[:, off[r] + c0:off[r] + c1]

    sent = [0]

    def send(i, dst):
        r, c0, c1, via = FLOWS[i]
        a, b = off[r] + c0, off[r] + c1
        m, n = engines(core, dst)
        rid, pid, _se = topo.addr(dst)
        if dst == root:
            g.remote_dma(T.land[:, a:b], stage(i), T.sem["grp%d" % group_of(a, b)], T.sem.sent, pid, rid, m)
        else:
            g.remote_dma(stage(i), stage(i), T.sem["f%d" % i], T.sem.sent, pid, rid, m)
        sent[0] += n

    if core == root:
        a = off[ROOT_RANK]
        w = widths[ROOT_RANK]
        g.dma_start(T.y[:, a:a + w], T.x[:, 0:w]).then_inc(T.sem.done_g, 16)
        need = [0] * len(GROUPS)
        for (r, c0, c1, via) in FLOWS:
            last = via[-1] if via else cores[r]
            need[group_of(off[r] + c0, off[r] + c1)] += engines(last, root)[1]
        n_h = 0
        for j, (ga, gb, qn) in enumerate(GROUPS):
            q = g.sync if qn == "sync" else g.scalar
            q.wait_ge(T.sem["grp%d" % j], need[j])
            q.dma_start(T.y[:, ga:gb], T.land[:, ga:gb]).then_inc(T.sem.done_h, 16)
            n_h += 16
        g.wait_ge(T.sem.done_g, 16)
        g.wait_ge(T.sem.done_h, n_h)
        return

    rank = T.rank_of(core)
    if rank is not None:
        mine = [i for i, f in enumerate(FLOWS) if f[0] == rank]
        for k, i in enumerate(mine):
            q = g.sync if k % 2 == 0 else g.scalar
            q.dma_start(stage(i), T.x[:, FLOWS[i][1]:FLOWS[i][2]]).then_inc(T.sem["ld%d" % k], 16)
        for k, i in enumerate(mine):
            g.wait_ge(T.sem["ld%d" % k], 16)
            send(i, FLOWS[i][3][0] if FLOWS[i][3] else root)
    else:
        for i, (r, c0, c1, via) in enumerate(FLOWS):
            if core in via:
                h = via.index(core)
                prev = via[h - 1] if h else cores[r]
                nxt = via[h + 1] if h + 1 < len(via) else root
                g.wait_ge(T.sem["f%d" % i], engines(prev, core)[1])
                send(i, nxt)
    if sent[0]:
        g.wait_ge(T.sem.sent, sent[0])
